import numpy as np
import ml_dtypes


def mxq(x, axis, fmt="e4m3"):
    dtype, down = {"e4m3": (ml_dtypes.float8_e4m3fn, 7), "e5m2": (ml_dtypes.float8_e5m2, 14)}[fmt]
    v = np.moveaxis(np.asarray(x, np.float32).astype(ml_dtypes.bfloat16).astype(np.float64), axis, -1)
    blocks = v.reshape(v.shape[:-1] + (-1, 32))
    amax = np.abs(blocks).max(-1, keepdims=True)
    byte = np.maximum(np.where(amax > 0, np.frexp(amax)[1] - 1 + 127, 0) - down, 1)
    scale = np.exp2(byte - 127.0)
    codes = (blocks / scale).astype(np.float32).astype(dtype).astype(np.float64)
    return np.moveaxis((codes * scale).reshape(v.shape), -1, axis)


WIDE = False


def mx_kscale(k):
    if not WIDE:
        return np.ones(k)
    levels = np.array([10, -10, 5, -5, 0])
    if k % 512:
        return np.exp2(np.random.permutation(np.resize(levels, k // 32))).repeat(32)
    a = np.empty((k // 512, 16))
    for p in range(k // 512):
        a[p, :8] = np.random.permutation(np.resize(levels, 8))
        for g in range(8):
            far = levels[np.abs(levels - a[p, g]) >= 10]
            a[p, g + 8] = far[np.random.randint(len(far))]
    return np.exp2(a.ravel()).repeat(32)


def f64(x):
    return np.asarray(x).astype(np.float64)


def striped(idx):
    return np.tile(idx.reshape(-1, 16).T, (8, 1)).astype(np.uint16)


def unstriped(offs):
    return offs[:16].T.reshape(-1).astype(np.int64)


E2M1 = np.array([0.0, 0.5, 1.0, 1.5, 2.0, 3.0, 4.0, 6.0, -0.0, -0.5, -1.0, -1.5, -2.0, -3.0, -4.0, -6.0])


def pack_weight(w, fmt):
    k, n = w.shape
    w = f64(np.asarray(w, np.float32).astype(ml_dtypes.bfloat16)).reshape(k // 32, 32, n)
    amax = np.abs(w).max(1)
    if fmt == "e4m3":
        byte = np.frexp(amax)[1] - 1 + 127 - 7
    else:
        mant, ex = np.frexp(amax / 6.0)
        byte = np.where(mant > 0.5, ex, ex - 1) + 127
    byte = np.clip(np.where(amax > 0, byte, 1), 1, 254)
    scaled = (w * np.exp2(127.0 - byte)[:, None, :]).reshape(k, n).astype(np.float32)
    by_word = np.ascontiguousarray(scaled.reshape(k // 512, 128, 4, n).transpose(0, 1, 3, 2))
    if fmt == "e4m3":
        words = by_word.astype(ml_dtypes.float8_e4m3fn).view(np.uint8)
    else:
        c = by_word.astype(ml_dtypes.float4_e2m1fn).view(np.uint8) & 0xF
        words = (c[..., 0::2] | (c[..., 1::2] << 4)).reshape(k // 512, 128, 2 * n)
    return np.ascontiguousarray(words), np.ascontiguousarray(byte.astype(np.uint8).reshape(k // 512, 16, n))


def unpack_weight(words, scales, fmt):
    g, _, n = scales.shape
    words = np.ascontiguousarray(words).reshape(g, 128, n, -1)
    if fmt == "e4m3":
        vals = words.view(ml_dtypes.float8_e4m3fn).astype(np.float64)
    else:
        nib = np.empty((g, 128, n, 4), np.uint8)
        nib[..., 0::2] = words & 0xF
        nib[..., 1::2] = words >> 4
        vals = E2M1[nib]
    vals = vals * np.repeat(np.exp2(scales.astype(np.float64) - 127.0), 8, axis=1)[..., None]
    return vals.transpose(0, 1, 3, 2).reshape(g * 512, n)


def gelu(v):
    return 0.5 * v * (1.0 + np.tanh(np.sqrt(2.0 / np.pi) * (v + 0.044715 * v**3)))


T, S, K, H, N, P1, P2, P3 = 4096, 2048, 1024, 1024, 512, 1024, 512, 256


def setup_inputs():
    n = np.random.standard_normal
    s = mx_kscale(K)[:, None]
    u = mx_kscale(H)[:, None]
    tab_words, tab_scales = pack_weight(n((K, T)) * s, "e4m3")
    w1_words, w1_scales = pack_weight(2.5 * n((K, H)) / np.sqrt(K) / s, "e2m1")
    return {
        "tab_words": tab_words, "tab_scales": tab_scales,
        "offs": striped(np.random.permutation(T)[:S]),
        "pos1": striped(np.random.permutation(S)[:P1]),
        "pos2": striped(np.random.permutation(S)[:P1]),
        "pos3": striped(np.random.permutation(P1)[:P2]),
        "pos4": striped(np.random.permutation(P1)[:P2]),
        "pos5": striped(np.random.permutation(P2)[:P3]),
        "pos6": striped(np.random.permutation(P2)[:P3]),
        "w1_words": w1_words, "w1_scales": w1_scales,
        "gain": (np.exp(0.3 * n(H)) * u[:, 0]).astype(np.float32),
        "w2": (2.0 * n((H, N)) / np.sqrt(H) / u).astype(np.float32),
        "bar": n((N, P3)).astype(np.float32),
    }


def reference(tab_words, tab_scales, offs, pos1, pos2, pos3, pos4, pos5, pos6,
              w1_words, w1_scales, gain, w2, bar):
    v = unpack_weight(tab_words, tab_scales, "e4m3")[:, unstriped(offs)]
    w1 = unpack_weight(w1_words, w1_scales, "e2m1")
    h = 1.0 / (1.0 + np.exp(-(w1.T @ v)))
    left = h[:, unstriped(pos1)]
    a1 = left * np.abs(left - h[:, unstriped(pos2)])
    a2 = np.maximum(a1[:, unstriped(pos3)], a1[:, unstriped(pos4)])
    a3 = f64(gain)[:, None] * (a2[:, unstriped(pos5)] + a2[:, unstriped(pos6)])
    y = mxq(f64(w2), 0, "e4m3").T @ mxq(a3, 0, "e4m3")
    return np.maximum(y, f64(bar))

@@ -1,0 +1,217 @@
+from contextlib import ExitStack
+
+import concourse.mybir as mybir
+
+T, S, K, H, N, P1, P2, P3 = 4096, 2048, 1024, 1024, 512, 1024, 512, 256
+FLOPS = 2 * K * H * S + 2 * H * N * P3
+
+F32 = mybir.dt.float32
+BF16 = mybir.dt.bfloat16
+I32 = mybir.dt.int32
+U32 = mybir.dt.uint32
+U16 = mybir.dt.uint16
+U8 = mybir.dt.uint8
+FP8X4 = mybir.dt.float8_e4m3fn_x4
+FP4X4 = mybir.dt.float4_e2m1fn_x4
+ALU = mybir.AluOpType
+ACT = mybir.ActivationFunctionType
+
+P = 128
+PACK = 4
+PASSES = 2
+BANK = 512
+SLOTS = H // P
+SLICES = S // BANK
+
+
+def tile_list_promotion_board_reports_kernel(
+    tc, tab_words, tab_scales, offs, pos1, pos2, pos3, pos4, pos5, pos6,
+    w1_words, w1_scales, gain, w2, bar, out,
+):
+    nc = tc.nc
+    with ExitStack() as ctx:
+        keep = ctx.enter_context(tc.tile_pool(name="keep", bufs=1))
+        ring = ctx.enter_context(tc.tile_pool(name="ring", bufs=3))
+        psum = ctx.enter_context(tc.psum_pool(name="psum", bufs=1))
+
+        def load_list(name, src):
+            tile = keep.tile(list(src.shape), U16, name=name)
+            nc.sync.dma_start(tile[:], src)
+            return tile
+
+        tab_sc = keep.tile([P, T], U8, name="tab_sc")
+        nc.sync.dma_start(tab_sc[0:32, :].bitcast(I32), tab_scales.rearrange("a q t -> (a q) t").bitcast(I32))
+        idx = load_list("idx", offs)
+        tab_w = [keep.tile([P, T], I32, name=f"tab_w{a}", tag=f"big{a}") for a in range(PASSES)]
+        nc.sync.dma_start(tab_w[0][:], tab_words[0].rearrange("p t i -> p (t i)").bitcast(I32))
+        p1, p2, p3, p4, p5, p6 = (
+            load_list(f"p{n + 1}", src) for n, src in enumerate((pos1, pos2, pos3, pos4, pos5, pos6))
+        )
+        nc.sync.dma_start(tab_w[1][:], tab_words[1].rearrange("p t i -> p (t i)").bitcast(I32))
+        w1_raw = keep.tile([P, PASSES, 2 * H], U8, name="w1_raw")
+        nc.sync.dma_start(w1_raw[:].bitcast(I32), w1_words.rearrange("a p c -> p a c").bitcast(I32))
+
+        w1_sc_raw = keep.tile([P, PASSES, H], U8, name="w1_sc_raw")
+        nc.gpsimd.memset(w1_sc_raw[:].bitcast(I32), 0)
+        for q in range(4):
+            nc.gpsimd.dma_start(
+                w1_sc_raw[32 * q : 32 * q + 4, :, :].bitcast(I32),
+                w1_scales[:, 4 * q : 4 * q + 4, :].rearrange("a r c -> r a c").bitcast(I32),
+            )
+
+        nc.vector.memset(tab_sc[32:64, :].bitcast(I32), 0)
+        nc.vector.memset(tab_sc[64:128, :].bitcast(I32), 0)
+        v_sc = keep.tile([P, PASSES, S], U8, name="v_sc", align_bytes=64)
+        nc.vector.memset(v_sc[:].bitcast(I32), 0)
+
+        picked_sc = keep.tile([P, S], U8, name="picked_sc", tag="picked")
+        nc.vector.tensor_copy(picked_sc[:], tab_sc[:].indirect(idx[:]))
+        for a in range(PASSES):
+            for q in range(4):
+                row = 16 * a + 4 * q
+                nc.scalar.dma_start(
+                    v_sc[32 * q : 32 * q + 4, a, :].bitcast(I32), picked_sc[row : row + 4, :].bitcast(I32)
+                )
+        v0 = keep.tile([P, S], U32, name="v0", align_bytes=64)
+        nc.vector.tensor_copy(v0[:], tab_w[0][:].bitcast(U32).indirect(idx[:]))
+
+        w1_w = keep.tile([P, PASSES, SLOTS, 2 * P], U8, name="w1_w", align_bytes=64)
+        w1_sc = keep.tile([P, PASSES, SLOTS, P], U8, name="w1_sc", align_bytes=64)
+
+        def deal_w1(slots):
+            for dst, src, run in ((w1_w, w1_raw, 4), (w1_sc, w1_sc_raw, 2)):
+                nc.vector.tensor_copy(
+                    dst[:].bitcast(I32).rearrange("p a s (g w) -> p a s g w", w=run)[:, :, slots],
+                    src[:].bitcast(I32).rearrange("p a (g s w) -> p a s g w", s=SLOTS, w=run)[:, :, slots],
+                )
+
+        v1 = []
+        for c in range(SLICES):
+            piece = keep.tile([P, BANK], U32, name=f"v1_{c}", align_bytes=64)
+            cols = BANK // 16
+            nc.vector.tensor_copy(piece[:], tab_w[1][:].bitcast(U32).indirect(idx[:, c * cols : (c + 1) * cols]))
+            v1.append(piece)
+            if c == 0:
+                deal_w1(slice(0, 1))
+        deal_w1(slice(1, SLOTS))
+
+        w2_raw = keep.tile([P, SLOTS, N], F32, name="w2_raw", tag="big0")
+        w2_rows = w2.rearrange("(g s e) n -> s g e n", s=SLOTS, e=8)
+        for s in range(SLOTS):
+            nc.sync.dma_start(w2_raw[:, s, :], w2_rows[s])
+        gain_t = keep.tile([P, SLOTS], F32, name="gain_t", tag="big1")
+        gain_rows = gain.rearrange("(g s e) -> e g s", s=SLOTS, e=8)
+        with nc.allow_non_contiguous_dma(reason="one gain value for each partition and slot"):
+            for e in range(8):
+                nc.sync.dma_start(gain_t[e:P:8, :], gain_rows[e])
+        bar_t = keep.tile([P, N // P, P3], F32, name="bar_t", tag="picked")
+        nc.sync.dma_start(bar_t[:], bar.rearrange("(m p) j -> p m j", p=P))
+
+        w2_w = [keep.tile([P, N], U32, name=f"w2_w{b}", align_bytes=64) for b in range(PASSES)]
+        w2_sc = [keep.tile([P, N], U8, name=f"w2_sc{b}", align_bytes=64) for b in range(PASSES)]
+
+        def quantise_w2(b):
+            woven = keep.tile([P, N, PACK], BF16, name=f"w2_woven{b}", align_bytes=64)
+            for m in range(N // P):
+                cols = slice(m * P, (m + 1) * P)
+                nc.scalar.copy(
+                    woven[:, cols, :].rearrange("p (c i) t -> p c t i", i=4),
+                    w2_raw[:, PACK * b : PACK * (b + 1), cols].rearrange("p t (c i) -> p c t i", i=4),
+                )
+            nc.vector.quantize_mx(
+                out=w2_w[b][:].bitcast(FP8X4), scales=w2_sc[b][:], in_=woven[:].rearrange("p n t -> p (n t)")
+            )
+
+        a3 = [keep.tile([P, P3, PACK], BF16, name=f"a3_{b}", align_bytes=64) for b in range(PASSES)]
+        y = [psum.tile([P, 2, P3], F32, name=f"y{m}") for m in range(2)]
+
+        def second_product(b):
+            a3_w = keep.tile([P, P3], U32, name=f"a3_w{b}", align_bytes=64)
+            a3_sc = keep.tile([P, P3], U8, name=f"a3_sc{b}", align_bytes=64)
+            nc.vector.quantize_mx(
+                out=a3_w[:].bitcast(FP8X4), scales=a3_sc[:], in_=a3[b][:].rearrange("p j t -> p (j t)")
+            )
+            for m in range(N // P):
+                cols = slice(m * P, (m + 1) * P)
+                nc.tensor.matmul_mx(
+                    out=y[m // 2][:, m % 2, :],
+                    lhsT=w2_w[b][:, cols].bitcast(FP8X4), lhsT_scale=w2_sc[b][:, cols],
+                    rhs=a3_w[:].bitcast(FP8X4), rhs_scale=a3_sc[:],
+                    start=(b == 0 and m % 2 == 0), stop=(b == PASSES - 1 and m % 2 == 1),
+                )
+
+        h, left, diff, dist, a1, first, second, a2, one = {}, {}, {}, {}, {}, {}, {}, {}, {}
+
+        def first_product(s):
+            h[s] = ring.tile([P, S], F32, name="h")
+            for c in range(SLICES):
+                cols = slice(c * BANK, (c + 1) * BANK)
+                acc = psum.tile([P, BANK], F32, name="acc", bufs=4)
+                for a in range(PASSES):
+                    words = v0[:, cols] if a == 0 else v1[c][:]
+                    nc.tensor.matmul_mx(
+                        out=acc[:],
+                        lhsT=w1_w[:, a, s, :].bitcast(FP4X4), lhsT_scale=w1_sc[:, a, s, :],
+                        rhs=words.bitcast(FP8X4), rhs_scale=v_sc[:, a, cols],
+                        start=(a == 0), stop=(a == PASSES - 1),
+                    )
+                nc.scalar.activation(h[s][:, cols], acc[:], ACT.Sigmoid)
+
+        def pick_left(s):
+            left[s] = ring.tile([P, P1], F32, name="left")
+            nc.vector.tensor_copy(left[s][:], h[s][:].indirect(p1[:]))
+
+        def pick_right(s):
+            diff[s] = ring.tile([P, P1], F32, name="diff")
+            nc.vector.tensor_tensor(diff[s][:], h[s][:].indirect(p2[:]), left[s][:], ALU.subtract)
+            dist[s] = ring.tile([P, P1], F32, name="dist")
+            nc.scalar.activation(dist[s][:], diff[s][:], ACT.Abs)
+
+        def join(s):
+            a1[s] = ring.tile([P, P1], F32, name="a1")
+            nc.vector.tensor_tensor(a1[s][:], left[s][:], dist[s][:], ALU.mult)
+
+        def pick_first(s):
+            first[s] = ring.tile([P, P2], F32, name="first")
+            nc.vector.tensor_copy(first[s][:], a1[s][:].indirect(p3[:]))
+
+        def pick_second(s):
+            second[s] = ring.tile([P, P2], F32, name="second")
+            nc.vector.tensor_copy(second[s][:], a1[s][:].indirect(p4[:]))
+
+        def larger(s):
+            a2[s] = ring.tile([P, P2], F32, name="a2")
+            nc.vector.tensor_tensor(a2[s][:], first[s][:], second[s][:], ALU.max)
+
+        def pick_one(s):
+            one[s] = ring.tile([P, P3], F32, name="one")
+            nc.vector.tensor_copy(one[s][:], a2[s][:].indirect(p5[:]))
+
+        def add_other(s):
+            both = ring.tile([P, P3], F32, name="both")
+            nc.vector.tensor_tensor(both[:], a2[s][:].indirect(p6[:]), one[s][:], ALU.add)
+            nc.scalar.activation(a3[s // PACK][:, :, s % PACK], both[:], ACT.Copy, scale=gain_t[:, s : s + 1])
+
+        steps = (
+            (pick_left, 0), (join, 1), (pick_right, 0), (pick_first, 1),
+            (pick_one, 2), (pick_second, 1), (add_other, 2), (larger, 1),
+        )
+        first_product(0)
+        for rnd in range(SLOTS + 2):
+            if rnd + 1 < SLOTS:
+                first_product(rnd + 1)
+            for step, lag in steps:
+                if 0 <= rnd - lag < SLOTS:
+                    step(rnd - lag)
+            if rnd in (2, 3):
+                quantise_w2(rnd - 2)
+            if rnd == PACK + 2:
+                second_product(0)
+        second_product(1)
+
+        out_rows = out.rearrange("(m p) j -> p m j", p=P)
+        for half in range(2):
+            rows = slice(2 * half, 2 * half + 2)
+            res = keep.tile([P, 2, P3], F32, name=f"res{half}")
+            nc.vector.tensor_tensor(res[:], y[half][:], bar_t[:, rows, :], ALU.max)
+            nc.sync.dma_start(out_rows[:, rows, :], res[:])

@@ -1,6 +1,7 @@
 from contextlib import ExitStack
 
 import concourse.mybir as mybir
+from concourse.masks import make_identity
 
 T, S, K, H, N, P1, P2, P3 = 4096, 2048, 1024, 1024, 512, 1024, 512, 256
 FLOPS = 2 * K * H * S + 2 * H * N * P3
@@ -42,14 +43,14 @@ def tile_list_promotion_board_reports_kernel(
         tab_sc = keep.tile([P, T], U8, name="tab_sc")
         nc.sync.dma_start(tab_sc[0:32, :].bitcast(I32), tab_scales.rearrange("a q t -> (a q) t").bitcast(I32))
         idx = load_list("idx", offs)
-        tab_w = [keep.tile([P, T], I32, name=f"tab_w{a}", tag=f"big{a}") for a in range(PASSES)]
+        w1_raw = keep.tile([P, PASSES, 2 * H], U8, name="w1_raw", tag="weights")
+        nc.sync.dma_start(w1_raw[:].bitcast(I32), w1_words.rearrange("a p c -> p a c").bitcast(I32))
+        tab_w = [keep.tile([P, T], I32, name=f"tab_w{a}", tag=f"big{a}", align_bytes=64) for a in range(PASSES)]
         nc.sync.dma_start(tab_w[0][:], tab_words[0].rearrange("p t i -> p (t i)").bitcast(I32))
         p1, p2, p3, p4, p5, p6 = (
             load_list(f"p{n + 1}", src) for n, src in enumerate((pos1, pos2, pos3, pos4, pos5, pos6))
         )
         nc.sync.dma_start(tab_w[1][:], tab_words[1].rearrange("p t i -> p (t i)").bitcast(I32))
-        w1_raw = keep.tile([P, PASSES, 2 * H], U8, name="w1_raw")
-        nc.sync.dma_start(w1_raw[:].bitcast(I32), w1_words.rearrange("a p c -> p a c").bitcast(I32))
 
         w1_sc_raw = keep.tile([P, PASSES, H], U8, name="w1_sc_raw")
         nc.gpsimd.memset(w1_sc_raw[:].bitcast(I32), 0)
@@ -61,8 +62,11 @@ def tile_list_promotion_board_reports_kernel(
 
         nc.vector.memset(tab_sc[32:64, :].bitcast(I32), 0)
         nc.vector.memset(tab_sc[64:128, :].bitcast(I32), 0)
-        v_sc = keep.tile([P, PASSES, S], U8, name="v_sc", align_bytes=64)
-        nc.vector.memset(v_sc[:].bitcast(I32), 0)
+        v_sc = [keep.tile([P, S], U8, name=f"v_sc{a}", align_bytes=64) for a in range(PASSES)]
+        for a in range(PASSES):
+            nc.gpsimd.memset(v_sc[a][:].bitcast(I32), 0)
+        ident = keep.tile([P, P], F32, name="ident")
+        make_identity(nc, ident[:])
 
         picked_sc = keep.tile([P, S], U8, name="picked_sc", tag="picked")
         nc.vector.tensor_copy(picked_sc[:], tab_sc[:].indirect(idx[:]))
@@ -70,20 +74,26 @@ def tile_list_promotion_board_reports_kernel(
             for q in range(4):
                 row = 16 * a + 4 * q
                 nc.scalar.dma_start(
-                    v_sc[32 * q : 32 * q + 4, a, :].bitcast(I32), picked_sc[row : row + 4, :].bitcast(I32)
+                    v_sc[a][32 * q : 32 * q + 4, :].bitcast(I32), picked_sc[row : row + 4, :].bitcast(I32)
                 )
         v0 = keep.tile([P, S], U32, name="v0", align_bytes=64)
         nc.vector.tensor_copy(v0[:], tab_w[0][:].bitcast(U32).indirect(idx[:]))
 
-        w1_w = keep.tile([P, PASSES, SLOTS, 2 * P], U8, name="w1_w", align_bytes=64)
         w1_sc = keep.tile([P, PASSES, SLOTS, P], U8, name="w1_sc", align_bytes=64)
+        nc.vector.tensor_copy(
+            w1_sc[:].bitcast(I32).rearrange("p a s (g w) -> p a s g w", w=2),
+            w1_sc_raw[:].bitcast(I32).rearrange("p a (g s w) -> p a s g w", s=SLOTS, w=2),
+        )
 
-        def deal_w1(slots):
-            for dst, src, run in ((w1_w, w1_raw, 4), (w1_sc, w1_sc_raw, 2)):
-                nc.vector.tensor_copy(
-                    dst[:].bitcast(I32).rearrange("p a s (g w) -> p a s g w", w=run)[:, :, slots],
-                    src[:].bitcast(I32).rearrange("p a (g s w) -> p a s g w", s=SLOTS, w=run)[:, :, slots],
-                )
+        def deal_w1(slots, name, tag):
+            dealt = keep.tile([P, PASSES, len(slots), 2 * P], U8, name=name, tag=tag, align_bytes=64)
+            nc.vector.tensor_copy(
+                dealt[:].bitcast(I32).rearrange("p a s (g w) -> p a s g w", w=4),
+                w1_raw[:].bitcast(I32).rearrange("p a (g s w) -> p a s g w", s=SLOTS, w=4)[:, :, slots.start : slots.stop],
+            )
+            return [[dealt[:, a, s - slots.start, :] for a in range(PASSES)] for s in slots]
+
+        w1_w = deal_w1(range(0, 1), "w1_first", "w1_first")
 
         v1 = []
         for c in range(SLICES):
@@ -91,15 +101,13 @@ def tile_list_promotion_board_reports_kernel(
             cols = BANK // 16
             nc.vector.tensor_copy(piece[:], tab_w[1][:].bitcast(U32).indirect(idx[:, c * cols : (c + 1) * cols]))
             v1.append(piece)
-            if c == 0:
-                deal_w1(slice(0, 1))
-        deal_w1(slice(1, SLOTS))
+        w1_w = w1_w + deal_w1(range(1, SLOTS), "w1_rest", "big1")
 
-        w2_raw = keep.tile([P, SLOTS, N], F32, name="w2_raw", tag="big0")
+        w2_raw = keep.tile([P, SLOTS, N], F32, name="w2_raw", tag="weights")
         w2_rows = w2.rearrange("(g s e) n -> s g e n", s=SLOTS, e=8)
         for s in range(SLOTS):
             nc.sync.dma_start(w2_raw[:, s, :], w2_rows[s])
-        gain_t = keep.tile([P, SLOTS], F32, name="gain_t", tag="big1")
+        gain_t = keep.tile([P, SLOTS], F32, name="gain_t", tag="big0", align_bytes=64)
         gain_rows = gain.rearrange("(g s e) -> e g s", s=SLOTS, e=8)
         with nc.allow_non_contiguous_dma(reason="one gain value for each partition and slot"):
             for e in range(8):
@@ -122,57 +130,80 @@ def tile_list_promotion_board_reports_kernel(
                 out=w2_w[b][:].bitcast(FP8X4), scales=w2_sc[b][:], in_=woven[:].rearrange("p n t -> p (n t)")
             )
 
-        a3 = [keep.tile([P, P3, PACK], BF16, name=f"a3_{b}", align_bytes=64) for b in range(PASSES)]
-        y = [psum.tile([P, 2, P3], F32, name=f"y{m}") for m in range(2)]
+        a3 = {}
+        y = []
 
         def second_product(b):
-            a3_w = keep.tile([P, P3], U32, name=f"a3_w{b}", align_bytes=64)
-            a3_sc = keep.tile([P, P3], U8, name=f"a3_sc{b}", align_bytes=64)
-            nc.vector.quantize_mx(
-                out=a3_w[:].bitcast(FP8X4), scales=a3_sc[:], in_=a3[b][:].rearrange("p j t -> p (j t)")
-            )
-            for m in range(N // P):
-                cols = slice(m * P, (m + 1) * P)
-                nc.tensor.matmul_mx(
-                    out=y[m // 2][:, m % 2, :],
-                    lhsT=w2_w[b][:, cols].bitcast(FP8X4), lhsT_scale=w2_sc[b][:, cols],
-                    rhs=a3_w[:].bitcast(FP8X4), rhs_scale=a3_sc[:],
-                    start=(b == 0 and m % 2 == 0), stop=(b == PASSES - 1 and m % 2 == 1),
+            if b == 0:
+                y.extend(psum.tile([P, N // P, P], F32, name=f"y{half}", tag="acc", bufs=4) for half in range(2))
+            for half in range(2):
+                a3_w = keep.tile([P, P], U32, name=f"a3_w{b}{half}", align_bytes=64)
+                a3_sc = keep.tile([P, P], U8, name=f"a3_sc{b}{half}", align_bytes=64)
+                nc.vector.quantize_mx(
+                    out=a3_w[:].bitcast(FP8X4), scales=a3_sc[:], in_=a3[b, half][:].rearrange("p j t -> p (j t)")
                 )
+                for m in range(N // P):
+                    cols = slice(m * P, (m + 1) * P)
+                    nc.tensor.matmul_mx(
+                        out=y[half][:, m, :],
+                        lhsT=w2_w[b][:, cols].bitcast(FP8X4), lhsT_scale=w2_sc[b][:, cols],
+                        rhs=a3_w[:].bitcast(FP8X4), rhs_scale=a3_sc[:],
+                        start=(b == 0 and m == 0), stop=(b == PASSES - 1 and m == N // P - 1),
+                    )
 
-        h, left, diff, dist, a1, first, second, a2, one = {}, {}, {}, {}, {}, {}, {}, {}, {}
+        h, left, square, a1, first, second, a2, one, both = {}, {}, {}, {}, {}, {}, {}, {}, {}
 
         def first_product(s):
             h[s] = ring.tile([P, S], F32, name="h")
             for c in range(SLICES):
                 cols = slice(c * BANK, (c + 1) * BANK)
-                acc = psum.tile([P, BANK], F32, name="acc", bufs=4)
+                acc = psum.tile([P, BANK], F32, name="acc", tag="acc", bufs=4)
                 for a in range(PASSES):
                     words = v0[:, cols] if a == 0 else v1[c][:]
                     nc.tensor.matmul_mx(
                         out=acc[:],
-                        lhsT=w1_w[:, a, s, :].bitcast(FP4X4), lhsT_scale=w1_sc[:, a, s, :],
-                        rhs=words.bitcast(FP8X4), rhs_scale=v_sc[:, a, cols],
+                        lhsT=w1_w[s][a].bitcast(FP4X4), lhsT_scale=w1_sc[:, a, s, :],
+                        rhs=words.bitcast(FP8X4), rhs_scale=v_sc[a][:, cols],
                         start=(a == 0), stop=(a == PASSES - 1),
                     )
                 nc.scalar.activation(h[s][:, cols], acc[:], ACT.Sigmoid)
 
-        def pick_left(s):
-            left[s] = ring.tile([P, P1], F32, name="left")
-            nc.vector.tensor_copy(left[s][:], h[s][:].indirect(p1[:]))
+        def pick_left(s, half):
+            if half == 0:
+                left[s] = keep.tile([P, P1], F32, name="left", tag=f"picks{s % 2}")
+                square[s] = ring.tile([P, P1], F32, name="square")
+            cols = slice(half * BANK, (half + 1) * BANK)
+            places = p1[:, half * BANK // 16 : (half + 1) * BANK // 16]
+            nc.vector.tensor_scalar(left[s][:, cols], h[s][:].indirect(places), -1.0, 0.0, ALU.mult, ALU.add)
+            nc.scalar.activation(square[s][:, cols], left[s][:, cols], ACT.Square)
 
         def pick_right(s):
-            diff[s] = ring.tile([P, P1], F32, name="diff")
-            nc.vector.tensor_tensor(diff[s][:], h[s][:].indirect(p2[:]), left[s][:], ALU.subtract)
-            dist[s] = ring.tile([P, P1], F32, name="dist")
-            nc.scalar.activation(dist[s][:], diff[s][:], ACT.Abs)
-
-        def join(s):
-            a1[s] = ring.tile([P, P1], F32, name="a1")
-            nc.vector.tensor_tensor(a1[s][:], left[s][:], dist[s][:], ALU.mult)
+            cross = keep.tile([P, P1], F32, name="cross", tag=f"joins{s % 2}")
+            nc.vector.tensor_tensor(cross[:], h[s][:].indirect(p2[:]), left[s][:], ALU.mult)
+            turned = [
+                keep.tile([P, BANK], F32, name="turned", tag=f"turned{s % 3}{half}", align_bytes=64) for half in range(2)
+            ]
+            a1[s] = keep.tile([P, P1], F32, name="a1", tag=f"joins{s % 2}")
+            for half in range(2):
+                cols = slice(half * BANK, (half + 1) * BANK)
+                there = psum.tile([P, PACK, P], F32, name="there", bufs=2)
+                for n, term in enumerate((square[s], cross)):
+                    for c in range(PACK):
+                        blk = slice(half * BANK + c * P, half * BANK + (c + 1) * P)
+                        nc.tensor.matmul(
+                            there[:, c, :], term[:, blk], ident[:], is_transpose=True,
+                            start=(n == 0 and c == 0), stop=(n == 1 and c == PACK - 1),
+                        )
+                nc.scalar.activation(turned[half][:], there[:].rearrange("p c r -> p (c r)"), ACT.Abs)
+            for half in range(2):
+                cols = slice(half * BANK, (half + 1) * BANK)
+                back = psum.tile([P, PACK, P], F32, name="back", bufs=2)
+                for c in range(PACK):
+                    nc.tensor.transpose(back[:, c, :], turned[half][:, c * P : (c + 1) * P], ident[:])
+                nc.scalar.copy(a1[s][:, cols], back[:].rearrange("p c r -> p (c r)"))
 
         def pick_first(s):
-            first[s] = ring.tile([P, P2], F32, name="first")
+            first[s] = keep.tile([P, P2], F32, name="first", tag=f"picks{(s + 1) % 2}")
             nc.vector.tensor_copy(first[s][:], a1[s][:].indirect(p3[:]))
 
         def pick_second(s):
@@ -185,16 +216,31 @@ def tile_list_promotion_board_reports_kernel(
 
         def pick_one(s):
             one[s] = ring.tile([P, P3], F32, name="one")
-            nc.vector.tensor_copy(one[s][:], a2[s][:].indirect(p5[:]))
+            for half in range(2):
+                places = p5[:, half * P // 16 : (half + 1) * P // 16]
+                nc.vector.tensor_copy(one[s][:, half * P : (half + 1) * P], a2[s][:].indirect(places))
 
         def add_other(s):
-            both = ring.tile([P, P3], F32, name="both")
-            nc.vector.tensor_tensor(both[:], a2[s][:].indirect(p6[:]), one[s][:], ALU.add)
-            nc.scalar.activation(a3[s // PACK][:, :, s % PACK], both[:], ACT.Copy, scale=gain_t[:, s : s + 1])
+            both[s] = ring.tile([P, P3], F32, name="both", bufs=PACK)
+            for half in range(2):
+                cols = slice(half * P, (half + 1) * P)
+                places = p6[:, half * P // 16 : (half + 1) * P // 16]
+                nc.vector.tensor_tensor(both[s][:, cols], a2[s][:].indirect(places), one[s][:, cols], ALU.add)
+
+        def apply_gain(s, after):
+            b = s // PACK
+            for half in range(2):
+                if (b, half) not in a3:
+                    a3[b, half] = keep.tile(
+                        [P, P, PACK], BF16, name=f"a3_{b}{half}", tag=f"turned{after % 3}{half}", align_bytes=64
+                    )
+                nc.scalar.activation(
+                    a3[b, half][:, :, s % PACK], both[s][:, half * P : (half + 1) * P], ACT.Copy, scale=gain_t[:, s : s + 1]
+                )
 
         steps = (
-            (pick_left, 0), (join, 1), (pick_right, 0), (pick_first, 1),
-            (pick_one, 2), (pick_second, 1), (add_other, 2), (larger, 1),
+            (pick_first, 2), (pick_second, 2), (lambda s: pick_left(s, 0), 0), (larger, 2),
+            (lambda s: pick_left(s, 1), 0), (pick_one, 2), (pick_right, 0), (add_other, 2),
         )
         first_product(0)
         for rnd in range(SLOTS + 2):
@@ -203,15 +249,22 @@ def tile_list_promotion_board_reports_kernel(
             for step, lag in steps:
                 if 0 <= rnd - lag < SLOTS:
                     step(rnd - lag)
-            if rnd in (2, 3):
-                quantise_w2(rnd - 2)
-            if rnd == PACK + 2:
+            if rnd in (5, 6):
+                quantise_w2(rnd - 5)
+            if rnd == 5:
+                for s in range(PACK):
+                    apply_gain(s, 5)
+            if rnd == 7:
+                apply_gain(4, 7)
+            if rnd >= 7:
+                apply_gain(rnd - 2, 7)
+            if rnd == 7:
                 second_product(0)
         second_product(1)
 
         out_rows = out.rearrange("(m p) j -> p m j", p=P)
         for half in range(2):
-            rows = slice(2 * half, 2 * half + 2)
-            res = keep.tile([P, 2, P3], F32, name=f"res{half}")
-            nc.vector.tensor_tensor(res[:], y[half][:], bar_t[:, rows, :], ALU.max)
-            nc.sync.dma_start(out_rows[:, rows, :], res[:])
+            cols = slice(half * P, (half + 1) * P)
+            res = keep.tile([P, N // P, P], F32, name=f"res{half}")
+            nc.vector.tensor_tensor(res[:], y[half][:], bar_t[:, :, cols], ALU.max)
+            nc.sync.dma_start(out_rows[:, :, cols], res[:])

@@ -1,3 +1,4 @@
+import itertools
 from contextlib import ExitStack
 
 import concourse.mybir as mybir
@@ -43,16 +44,16 @@ def tile_list_promotion_board_reports_kernel(
         tab_sc = keep.tile([P, T], U8, name="tab_sc")
         nc.sync.dma_start(tab_sc[0:32, :].bitcast(I32), tab_scales.rearrange("a q t -> (a q) t").bitcast(I32))
         idx = load_list("idx", offs)
-        w1_raw = keep.tile([P, PASSES, 2 * H], U8, name="w1_raw", tag="weights")
-        nc.sync.dma_start(w1_raw[:].bitcast(I32), w1_words.rearrange("a p c -> p a c").bitcast(I32))
         tab_w = [keep.tile([P, T], I32, name=f"tab_w{a}", tag=f"big{a}", align_bytes=64) for a in range(PASSES)]
         nc.sync.dma_start(tab_w[0][:], tab_words[0].rearrange("p t i -> p (t i)").bitcast(I32))
+        w1_raw = keep.tile([P, PASSES, 2 * H], U8, name="w1_raw", tag="weights")
+        nc.sync.dma_start(w1_raw[:].bitcast(I32), w1_words.rearrange("a p c -> p a c").bitcast(I32))
+        nc.sync.dma_start(tab_w[1][:], tab_words[1].rearrange("p t i -> p (t i)").bitcast(I32))
         p1, p2, p3, p4, p5, p6 = (
             load_list(f"p{n + 1}", src) for n, src in enumerate((pos1, pos2, pos3, pos4, pos5, pos6))
         )
-        nc.sync.dma_start(tab_w[1][:], tab_words[1].rearrange("p t i -> p (t i)").bitcast(I32))
 
-        w1_sc_raw = keep.tile([P, PASSES, H], U8, name="w1_sc_raw")
+        w1_sc_raw = keep.tile([P, PASSES, H], U8, name="w1_sc_raw", tag="w1_sc_raw")
         nc.gpsimd.memset(w1_sc_raw[:].bitcast(I32), 0)
         for q in range(4):
             nc.gpsimd.dma_start(
@@ -79,7 +80,7 @@ def tile_list_promotion_board_reports_kernel(
         v0 = keep.tile([P, S], U32, name="v0", align_bytes=64)
         nc.vector.tensor_copy(v0[:], tab_w[0][:].bitcast(U32).indirect(idx[:]))
 
-        w1_sc = keep.tile([P, PASSES, SLOTS, P], U8, name="w1_sc", align_bytes=64)
+        w1_sc = keep.tile([P, PASSES, SLOTS, P], U8, name="w1_sc", tag="big0", align_bytes=64)
         nc.vector.tensor_copy(
             w1_sc[:].bitcast(I32).rearrange("p a s (g w) -> p a s g w", w=2),
             w1_sc_raw[:].bitcast(I32).rearrange("p a (g s w) -> p a s g w", s=SLOTS, w=2),
@@ -107,7 +108,7 @@ def tile_list_promotion_board_reports_kernel(
         w2_rows = w2.rearrange("(g s e) n -> s g e n", s=SLOTS, e=8)
         for s in range(SLOTS):
             nc.sync.dma_start(w2_raw[:, s, :], w2_rows[s])
-        gain_t = keep.tile([P, SLOTS], F32, name="gain_t", tag="big0", align_bytes=64)
+        gain_t = keep.tile([P, SLOTS], F32, name="gain_t", tag="w1_sc_raw")
         gain_rows = gain.rearrange("(g s e) -> e g s", s=SLOTS, e=8)
         with nc.allow_non_contiguous_dma(reason="one gain value for each partition and slot"):
             for e in range(8):
@@ -155,41 +156,41 @@ def tile_list_promotion_board_reports_kernel(
 
         def first_product(s):
             h[s] = ring.tile([P, S], F32, name="h")
-            for c in range(SLICES):
+            acc = [psum.tile([P, BANK], F32, name="acc", tag="acc", bufs=4) for c in range(SLICES)]
+            for c, a in itertools.product(range(SLICES), range(PASSES)):
                 cols = slice(c * BANK, (c + 1) * BANK)
-                acc = psum.tile([P, BANK], F32, name="acc", tag="acc", bufs=4)
-                for a in range(PASSES):
-                    words = v0[:, cols] if a == 0 else v1[c][:]
-                    nc.tensor.matmul_mx(
-                        out=acc[:],
-                        lhsT=w1_w[s][a].bitcast(FP4X4), lhsT_scale=w1_sc[:, a, s, :],
-                        rhs=words.bitcast(FP8X4), rhs_scale=v_sc[a][:, cols],
-                        start=(a == 0), stop=(a == PASSES - 1),
-                    )
-                nc.scalar.activation(h[s][:, cols], acc[:], ACT.Sigmoid)
+                words = v0[:, cols] if a == 0 else v1[c][:]
+                nc.tensor.matmul_mx(
+                    out=acc[c][:],
+                    lhsT=w1_w[s][a].bitcast(FP4X4), lhsT_scale=w1_sc[:, a, s, :],
+                    rhs=words.bitcast(FP8X4), rhs_scale=v_sc[a][:, cols],
+                    start=(a == 0), stop=(a == PASSES - 1),
+                )
+                if a == PASSES - 1:
+                    nc.scalar.activation(h[s][:, cols], acc[c][:], ACT.Sigmoid)
 
         def pick_left(s, half):
             if half == 0:
                 left[s] = keep.tile([P, P1], F32, name="left", tag=f"picks{s % 2}")
-                square[s] = ring.tile([P, P1], F32, name="square")
+            square[s, half] = keep.tile([P, BANK], F32, name="square", tag=f"square{s % 3}{half}", align_bytes=64)
             cols = slice(half * BANK, (half + 1) * BANK)
             places = p1[:, half * BANK // 16 : (half + 1) * BANK // 16]
             nc.vector.tensor_scalar(left[s][:, cols], h[s][:].indirect(places), -1.0, 0.0, ALU.mult, ALU.add)
-            nc.scalar.activation(square[s][:, cols], left[s][:, cols], ACT.Square)
+            nc.scalar.activation(square[s, half][:], left[s][:, cols], ACT.Square)
 
         def pick_right(s):
-            cross = keep.tile([P, P1], F32, name="cross", tag=f"joins{s % 2}")
+            cross = keep.tile([P, P1], F32, name="cross", tag=f"joins{s % 3}")
             nc.vector.tensor_tensor(cross[:], h[s][:].indirect(p2[:]), left[s][:], ALU.mult)
             turned = [
                 keep.tile([P, BANK], F32, name="turned", tag=f"turned{s % 3}{half}", align_bytes=64) for half in range(2)
             ]
-            a1[s] = keep.tile([P, P1], F32, name="a1", tag=f"joins{s % 2}")
+            a1[s] = keep.tile([P, P1], F32, name="a1", tag=f"joins{s % 3}")
             for half in range(2):
                 cols = slice(half * BANK, (half + 1) * BANK)
                 there = psum.tile([P, PACK, P], F32, name="there", bufs=2)
-                for n, term in enumerate((square[s], cross)):
+                for n, term in enumerate((square[s, half][:], cross[:, cols])):
                     for c in range(PACK):
-                        blk = slice(half * BANK + c * P, half * BANK + (c + 1) * P)
+                        blk = slice(c * P, (c + 1) * P)
                         nc.tensor.matmul(
                             there[:, c, :], term[:, blk], ident[:], is_transpose=True,
                             start=(n == 0 and c == 0), stop=(n == 1 and c == PACK - 1),
@@ -203,7 +204,7 @@ def tile_list_promotion_board_reports_kernel(
                 nc.scalar.copy(a1[s][:, cols], back[:].rearrange("p c r -> p (c r)"))
 
         def pick_first(s):
-            first[s] = keep.tile([P, P2], F32, name="first", tag=f"picks{(s + 1) % 2}")
+            first[s] = keep.tile([P, P2], F32, name="first", tag=f"picks{s % 2}")
             nc.vector.tensor_copy(first[s][:], a1[s][:].indirect(p3[:]))
 
         def pick_second(s):
@@ -216,49 +217,46 @@ def tile_list_promotion_board_reports_kernel(
 
         def pick_one(s):
             one[s] = ring.tile([P, P3], F32, name="one")
-            for half in range(2):
-                places = p5[:, half * P // 16 : (half + 1) * P // 16]
-                nc.vector.tensor_copy(one[s][:, half * P : (half + 1) * P], a2[s][:].indirect(places))
+            nc.vector.tensor_copy(one[s][:], a2[s][:].indirect(p5[:]))
 
         def add_other(s):
-            both[s] = ring.tile([P, P3], F32, name="both", bufs=PACK)
-            for half in range(2):
-                cols = slice(half * P, (half + 1) * P)
-                places = p6[:, half * P // 16 : (half + 1) * P // 16]
+            both[s] = ring.tile([P, P3], F32, name="both", bufs=5)
+            width = P if s == SLOTS - 1 else P3
+            for j in range(0, P3, width):
+                cols = slice(j, j + width)
+                places = p6[:, j // 16 : (j + width) // 16]
                 nc.vector.tensor_tensor(both[s][:, cols], a2[s][:].indirect(places), one[s][:, cols], ALU.add)
 
-        def apply_gain(s, after):
+        def apply_gain(s):
             b = s // PACK
             for half in range(2):
                 if (b, half) not in a3:
-                    a3[b, half] = keep.tile(
-                        [P, P, PACK], BF16, name=f"a3_{b}{half}", tag=f"turned{after % 3}{half}", align_bytes=64
-                    )
+                    tag = ("square", "turned")[b] + f"{(SLOTS - 1) % 3}{half}"
+                    a3[b, half] = keep.tile([P, P, PACK], BF16, name=f"a3_{b}{half}", tag=tag, align_bytes=64)
                 nc.scalar.activation(
                     a3[b, half][:, :, s % PACK], both[s][:, half * P : (half + 1) * P], ACT.Copy, scale=gain_t[:, s : s + 1]
                 )
 
+        lag = 3
         steps = (
-            (pick_first, 2), (pick_second, 2), (lambda s: pick_left(s, 0), 0), (larger, 2),
-            (lambda s: pick_left(s, 1), 0), (pick_one, 2), (pick_right, 0), (add_other, 2),
+            (pick_first, lag), (pick_second, lag), (lambda s: pick_left(s, 0), 0), (larger, lag),
+            (lambda s: pick_left(s, 1), 0), (pick_one, lag), (pick_right, 0), (add_other, lag),
         )
         first_product(0)
-        for rnd in range(SLOTS + 2):
+        for rnd in range(SLOTS + lag):
             if rnd + 1 < SLOTS:
                 first_product(rnd + 1)
-            for step, lag in steps:
-                if 0 <= rnd - lag < SLOTS:
-                    step(rnd - lag)
-            if rnd in (5, 6):
-                quantise_w2(rnd - 5)
-            if rnd == 5:
+            for step, behind in steps:
+                if 0 <= rnd - behind < SLOTS:
+                    step(rnd - behind)
+            if rnd in (6, 7):
+                quantise_w2(rnd - 6)
+            if rnd == SLOTS - 1:
                 for s in range(PACK):
-                    apply_gain(s, 5)
-            if rnd == 7:
-                apply_gain(4, 7)
-            if rnd >= 7:
-                apply_gain(rnd - 2, 7)
-            if rnd == 7:
+                    apply_gain(s)
+            if rnd >= SLOTS - 1:
+                apply_gain(rnd - lag)
+            if rnd == SLOTS:
                 second_product(0)
         second_product(1)
 

@@ -42,59 +42,56 @@ def tile_list_promotion_board_reports_kernel(
             return tile
 
         tab_sc = keep.tile([P, T], U8, name="tab_sc")
-        nc.sync.dma_start(tab_sc[0:32, :].bitcast(I32), tab_scales.rearrange("a q t -> (a q) t").bitcast(I32))
+        nc.sync.dma_start(tab_sc[96:128, :].bitcast(I32), tab_scales.rearrange("a q t -> (a q) t").bitcast(I32))
         idx = load_list("idx", offs)
         tab_w = [keep.tile([P, T], I32, name=f"tab_w{a}", tag=f"big{a}", align_bytes=64) for a in range(PASSES)]
         nc.sync.dma_start(tab_w[0][:], tab_words[0].rearrange("p t i -> p (t i)").bitcast(I32))
-        w1_raw = keep.tile([P, PASSES, 2 * H], U8, name="w1_raw", tag="weights")
+        w1_raw = keep.tile([P, PASSES, 2 * H], U8, name="w1_raw", tag="weights", align_bytes=64)
         nc.sync.dma_start(w1_raw[:].bitcast(I32), w1_words.rearrange("a p c -> p a c").bitcast(I32))
         nc.sync.dma_start(tab_w[1][:], tab_words[1].rearrange("p t i -> p (t i)").bitcast(I32))
         p1, p2, p3, p4, p5, p6 = (
             load_list(f"p{n + 1}", src) for n, src in enumerate((pos1, pos2, pos3, pos4, pos5, pos6))
         )
 
+        nc.gpsimd.memset(tab_sc[0:96, :].bitcast(I32), 0)
+        ident = keep.tile([P, P], F32, name="ident")
+        make_identity(nc, ident[:])
         w1_sc_raw = keep.tile([P, PASSES, H], U8, name="w1_sc_raw", tag="w1_sc_raw")
-        nc.gpsimd.memset(w1_sc_raw[:].bitcast(I32), 0)
+        nc.vector.memset(w1_sc_raw[:].bitcast(I32), 0)
         for q in range(4):
             nc.gpsimd.dma_start(
                 w1_sc_raw[32 * q : 32 * q + 4, :, :].bitcast(I32),
                 w1_scales[:, 4 * q : 4 * q + 4, :].rearrange("a r c -> r a c").bitcast(I32),
             )
-
-        nc.vector.memset(tab_sc[32:64, :].bitcast(I32), 0)
-        nc.vector.memset(tab_sc[64:128, :].bitcast(I32), 0)
         v_sc = [keep.tile([P, S], U8, name=f"v_sc{a}", align_bytes=64) for a in range(PASSES)]
         for a in range(PASSES):
-            nc.gpsimd.memset(v_sc[a][:].bitcast(I32), 0)
-        ident = keep.tile([P, P], F32, name="ident")
-        make_identity(nc, ident[:])
+            nc.vector.memset(v_sc[a][:].bitcast(I32), 0)
+        minus_column = keep.tile([P, 1], F32, name="minus_column")
+        nc.vector.memset(minus_column[:], -1.0)
+        minus_one = keep.tile([P, P1], F32, name="minus_one")
+        nc.scalar.copy(minus_one[:], minus_column[:].to_broadcast([P, P1]))
 
         picked_sc = keep.tile([P, S], U8, name="picked_sc", tag="picked")
         nc.vector.tensor_copy(picked_sc[:], tab_sc[:].indirect(idx[:]))
         for a in range(PASSES):
             for q in range(4):
-                row = 16 * a + 4 * q
+                row = 96 + 16 * a + 4 * q
                 nc.scalar.dma_start(
                     v_sc[a][32 * q : 32 * q + 4, :].bitcast(I32), picked_sc[row : row + 4, :].bitcast(I32)
                 )
         v0 = keep.tile([P, S], U32, name="v0", align_bytes=64)
         nc.vector.tensor_copy(v0[:], tab_w[0][:].bitcast(U32).indirect(idx[:]))
 
-        w1_sc = keep.tile([P, PASSES, SLOTS, P], U8, name="w1_sc", tag="big0", align_bytes=64)
-        nc.vector.tensor_copy(
-            w1_sc[:].bitcast(I32).rearrange("p a s (g w) -> p a s g w", w=2),
-            w1_sc_raw[:].bitcast(I32).rearrange("p a (g s w) -> p a s g w", s=SLOTS, w=2),
-        )
-
-        def deal_w1(slots, name, tag):
-            dealt = keep.tile([P, PASSES, len(slots), 2 * P], U8, name=name, tag=tag, align_bytes=64)
+        def deal_w1(raw, run, slots, name, tag):
+            dealt = keep.tile([P, PASSES, len(slots), 64 * run], U8, name=name, tag=tag, align_bytes=64)
             nc.vector.tensor_copy(
-                dealt[:].bitcast(I32).rearrange("p a s (g w) -> p a s g w", w=4),
-                w1_raw[:].bitcast(I32).rearrange("p a (g s w) -> p a s g w", s=SLOTS, w=4)[:, :, slots.start : slots.stop],
+                dealt[:].bitcast(I32).rearrange("p a s (g w) -> p a s g w", w=run),
+                raw[:].bitcast(I32).rearrange("p a (g s w) -> p a s g w", s=SLOTS, w=run)[:, :, slots.start : slots.stop],
             )
             return [[dealt[:, a, s - slots.start, :] for a in range(PASSES)] for s in slots]
 
-        w1_w = deal_w1(range(0, 1), "w1_first", "w1_first")
+        w1_sc = deal_w1(w1_sc_raw, 2, range(0, 1), "w1_sc_first", "big0")
+        w1_w = deal_w1(w1_raw, 4, range(0, 1), "w1_first", "w1_first")
 
         v1 = []
         for c in range(SLICES):
@@ -102,13 +99,14 @@ def tile_list_promotion_board_reports_kernel(
             cols = BANK // 16
             nc.vector.tensor_copy(piece[:], tab_w[1][:].bitcast(U32).indirect(idx[:, c * cols : (c + 1) * cols]))
             v1.append(piece)
-        w1_w = w1_w + deal_w1(range(1, SLOTS), "w1_rest", "big1")
+        w1_w = w1_w + deal_w1(w1_raw, 4, range(1, SLOTS), "w1_rest", "big1")
+        w1_sc = w1_sc + deal_w1(w1_sc_raw, 2, range(1, SLOTS), "w1_sc_rest", "weights")
 
-        w2_raw = keep.tile([P, SLOTS, N], F32, name="w2_raw", tag="weights")
+        w2_raw = keep.tile([P, SLOTS, N], F32, name="w2_raw", tag="w1_sc_raw")
         w2_rows = w2.rearrange("(g s e) n -> s g e n", s=SLOTS, e=8)
         for s in range(SLOTS):
             nc.sync.dma_start(w2_raw[:, s, :], w2_rows[s])
-        gain_t = keep.tile([P, SLOTS], F32, name="gain_t", tag="w1_sc_raw")
+        gain_t = keep.tile([P, SLOTS], F32, name="gain_t", tag="big0", align_bytes=64)
         gain_rows = gain.rearrange("(g s e) -> e g s", s=SLOTS, e=8)
         with nc.allow_non_contiguous_dma(reason="one gain value for each partition and slot"):
             for e in range(8):
@@ -162,21 +160,19 @@ def tile_list_promotion_board_reports_kernel(
                 words = v0[:, cols] if a == 0 else v1[c][:]
                 nc.tensor.matmul_mx(
                     out=acc[c][:],
-                    lhsT=w1_w[s][a].bitcast(FP4X4), lhsT_scale=w1_sc[:, a, s, :],
+                    lhsT=w1_w[s][a].bitcast(FP4X4), lhsT_scale=w1_sc[s][a],
                     rhs=words.bitcast(FP8X4), rhs_scale=v_sc[a][:, cols],
                     start=(a == 0), stop=(a == PASSES - 1),
                 )
                 if a == PASSES - 1:
                     nc.scalar.activation(h[s][:, cols], acc[c][:], ACT.Sigmoid)
 
-        def pick_left(s, half):
-            if half == 0:
-                left[s] = keep.tile([P, P1], F32, name="left", tag=f"picks{s % 2}")
-            square[s, half] = keep.tile([P, BANK], F32, name="square", tag=f"square{s % 3}{half}", align_bytes=64)
-            cols = slice(half * BANK, (half + 1) * BANK)
-            places = p1[:, half * BANK // 16 : (half + 1) * BANK // 16]
-            nc.vector.tensor_scalar(left[s][:, cols], h[s][:].indirect(places), -1.0, 0.0, ALU.mult, ALU.add)
-            nc.scalar.activation(square[s, half][:], left[s][:, cols], ACT.Square)
+        def pick_left(s):
+            left[s] = keep.tile([P, P1], F32, name="left", tag=f"picks{s % 2}")
+            nc.vector.tensor_tensor(left[s][:], h[s][:].indirect(p1[:]), minus_one[:], ALU.mult)
+            for half in range(2):
+                square[s, half] = keep.tile([P, BANK], F32, name="square", tag=f"square{s % 3}{half}", align_bytes=64)
+                nc.scalar.activation(square[s, half][:], left[s][:, half * BANK : (half + 1) * BANK], ACT.Square)
 
         def pick_right(s):
             cross = keep.tile([P, P1], F32, name="cross", tag=f"joins{s % 3}")
@@ -205,7 +201,8 @@ def tile_list_promotion_board_reports_kernel(
 
         def pick_first(s):
             first[s] = keep.tile([P, P2], F32, name="first", tag=f"picks{s % 2}")
-            nc.vector.tensor_copy(first[s][:], a1[s][:].indirect(p3[:]))
+            for j in range(0, P2, P3):
+                nc.vector.tensor_copy(first[s][:, j : j + P3], a1[s][:].indirect(p3[:, j // 16 : (j + P3) // 16]))
 
         def pick_second(s):
             second[s] = ring.tile([P, P2], F32, name="second")
@@ -213,7 +210,9 @@ def tile_list_promotion_board_reports_kernel(
 
         def larger(s):
             a2[s] = ring.tile([P, P2], F32, name="a2")
-            nc.vector.tensor_tensor(a2[s][:], first[s][:], second[s][:], ALU.max)
+            for j in range(0, P2, P3):
+                cols = slice(j, j + P3)
+                nc.vector.tensor_tensor(a2[s][:, cols], first[s][:, cols], second[s][:, cols], ALU.max)
 
         def pick_one(s):
             one[s] = ring.tile([P, P3], F32, name="one")
@@ -239,8 +238,8 @@ def tile_list_promotion_board_reports_kernel(
 
         lag = 3
         steps = (
-            (pick_first, lag), (pick_second, lag), (lambda s: pick_left(s, 0), 0), (larger, lag),
-            (lambda s: pick_left(s, 1), 0), (pick_one, lag), (pick_right, 0), (add_other, lag),
+            (pick_second, lag), (pick_first, lag), (pick_left, 0), (larger, lag),
+            (pick_right, 0), (pick_one, lag), (add_other, lag),
         )
         first_product(0)
         for rnd in range(SLOTS + lag):

import itertools
from contextlib import ExitStack

import concourse.mybir as mybir
from concourse.masks import make_identity

T, S, K, H, N, P1, P2, P3 = 4096, 2048, 1024, 1024, 512, 1024, 512, 256
FLOPS = 2 * K * H * S + 2 * H * N * P3

F32 = mybir.dt.float32
BF16 = mybir.dt.bfloat16
I32 = mybir.dt.int32
U32 = mybir.dt.uint32
U16 = mybir.dt.uint16
U8 = mybir.dt.uint8
FP8X4 = mybir.dt.float8_e4m3fn_x4
FP4X4 = mybir.dt.float4_e2m1fn_x4
ALU = mybir.AluOpType
ACT = mybir.ActivationFunctionType

P = 128
PACK = 4
PASSES = 2
BANK = 512
SLOTS = H // P
SLICES = S // BANK


def tile_list_promotion_board_reports_kernel(
    tc, tab_words, tab_scales, offs, pos1, pos2, pos3, pos4, pos5, pos6,
    w1_words, w1_scales, gain, w2, bar, out,
):
    nc = tc.nc
    with ExitStack() as ctx:
        keep = ctx.enter_context(tc.tile_pool(name="keep", bufs=1))
        ring = ctx.enter_context(tc.tile_pool(name="ring", bufs=3))
        psum = ctx.enter_context(tc.psum_pool(name="psum", bufs=1))

        def load_list(name, src):
            tile = keep.tile(list(src.shape), U16, name=name)
            nc.sync.dma_start(tile[:], src)
            return tile

        tab_sc = keep.tile([P, T], U8, name="tab_sc")
        nc.sync.dma_start(tab_sc[96:128, :].bitcast(I32), tab_scales.rearrange("a q t -> (a q) t").bitcast(I32))
        idx = load_list("idx", offs)
        tab_w = [keep.tile([P, T], I32, name=f"tab_w{a}", tag=f"big{a}", align_bytes=64) for a in range(PASSES)]
        nc.sync.dma_start(tab_w[0][:], tab_words[0].rearrange("p t i -> p (t i)").bitcast(I32))
        w1_raw = keep.tile([P, PASSES, 2 * H], U8, name="w1_raw", tag="weights", align_bytes=64)
        nc.sync.dma_start(w1_raw[:].bitcast(I32), w1_words.rearrange("a p c -> p a c").bitcast(I32))
        nc.sync.dma_start(tab_w[1][:], tab_words[1].rearrange("p t i -> p (t i)").bitcast(I32))
        p1, p2, p3, p4, p5, p6 = (
            load_list(f"p{n + 1}", src) for n, src in enumerate((pos1, pos2, pos3, pos4, pos5, pos6))
        )

        nc.gpsimd.memset(tab_sc[0:96, :].bitcast(I32), 0)
        ident = keep.tile([P, P], F32, name="ident")
        make_identity(nc, ident[:])
        w1_sc_raw = keep.tile([P, PASSES, H], U8, name="w1_sc_raw", tag="w1_sc_raw")
        nc.vector.memset(w1_sc_raw[:].bitcast(I32), 0)
        for q in range(4):
            nc.gpsimd.dma_start(
                w1_sc_raw[32 * q : 32 * q + 4, :, :].bitcast(I32),
                w1_scales[:, 4 * q : 4 * q + 4, :].rearrange("a r c -> r a c").bitcast(I32),
            )
        v_sc = [keep.tile([P, S], U8, name=f"v_sc{a}", align_bytes=64) for a in range(PASSES)]
        for a in range(PASSES):
            nc.vector.memset(v_sc[a][:].bitcast(I32), 0)
        minus_column = keep.tile([P, 1], F32, name="minus_column")
        nc.vector.memset(minus_column[:], -1.0)
        minus_one = keep.tile([P, P1], F32, name="minus_one")
        nc.scalar.copy(minus_one[:], minus_column[:].to_broadcast([P, P1]))

        picked_sc = keep.tile([P, S], U8, name="picked_sc", tag="picked")
        nc.vector.tensor_copy(picked_sc[:], tab_sc[:].indirect(idx[:]))
        for a in range(PASSES):
            for q in range(4):
                row = 96 + 16 * a + 4 * q
                nc.scalar.dma_start(
                    v_sc[a][32 * q : 32 * q + 4, :].bitcast(I32), picked_sc[row : row + 4, :].bitcast(I32)
                )
        v0 = keep.tile([P, S], U32, name="v0", align_bytes=64)
        nc.vector.tensor_copy(v0[:], tab_w[0][:].bitcast(U32).indirect(idx[:]))

        def deal_w1(raw, run, slots, name, tag):
            dealt = keep.tile([P, PASSES, len(slots), 64 * run], U8, name=name, tag=tag, align_bytes=64)
            nc.vector.tensor_copy(
                dealt[:].bitcast(I32).rearrange("p a s (g w) -> p a s g w", w=run),
                raw[:].bitcast(I32).rearrange("p a (g s w) -> p a s g w", s=SLOTS, w=run)[:, :, slots.start : slots.stop],
            )
            return [[dealt[:, a, s - slots.start, :] for a in range(PASSES)] for s in slots]

        w1_sc = deal_w1(w1_sc_raw, 2, range(0, 1), "w1_sc_first", "big0")
        w1_w = deal_w1(w1_raw, 4, range(0, 1), "w1_first", "w1_first")

        v1 = []
        for c in range(SLICES):
            piece = keep.tile([P, BANK], U32, name=f"v1_{c}", align_bytes=64)
            cols = BANK // 16
            nc.vector.tensor_copy(piece[:], tab_w[1][:].bitcast(U32).indirect(idx[:, c * cols : (c + 1) * cols]))
            v1.append(piece)
        w1_w = w1_w + deal_w1(w1_raw, 4, range(1, SLOTS), "w1_rest", "big1")
        w1_sc = w1_sc + deal_w1(w1_sc_raw, 2, range(1, SLOTS), "w1_sc_rest", "weights")

        w2_raw = keep.tile([P, SLOTS, N], F32, name="w2_raw", tag="w1_sc_raw")
        w2_rows = w2.rearrange("(g s e) n -> s g e n", s=SLOTS, e=8)
        for s in range(SLOTS):
            nc.sync.dma_start(w2_raw[:, s, :], w2_rows[s])
        gain_t = keep.tile([P, SLOTS], F32, name="gain_t", tag="big0", align_bytes=64)
        gain_rows = gain.rearrange("(g s e) -> e g s", s=SLOTS, e=8)
        with nc.allow_non_contiguous_dma(reason="one gain value for each partition and slot"):
            for e in range(8):
                nc.sync.dma_start(gain_t[e:P:8, :], gain_rows[e])
        bar_t = keep.tile([P, N // P, P3], F32, name="bar_t", tag="picked")
        nc.sync.dma_start(bar_t[:], bar.rearrange("(m p) j -> p m j", p=P))

        w2_w = [keep.tile([P, N], U32, name=f"w2_w{b}", align_bytes=64) for b in range(PASSES)]
        w2_sc = [keep.tile([P, N], U8, name=f"w2_sc{b}", align_bytes=64) for b in range(PASSES)]

        def quantise_w2(b):
            woven = keep.tile([P, N, PACK], BF16, name=f"w2_woven{b}", align_bytes=64)
            for m in range(N // P):
                cols = slice(m * P, (m + 1) * P)
                nc.scalar.copy(
                    woven[:, cols, :].rearrange("p (c i) t -> p c t i", i=4),
                    w2_raw[:, PACK * b : PACK * (b + 1), cols].rearrange("p t (c i) -> p c t i", i=4),
                )
            nc.vector.quantize_mx(
                out=w2_w[b][:].bitcast(FP8X4), scales=w2_sc[b][:], in_=woven[:].rearrange("p n t -> p (n t)")
            )

        a3 = {}
        y = []

        def second_product(b):
            if b == 0:
                y.extend(psum.tile([P, N // P, P], F32, name=f"y{half}", tag="acc", bufs=4) for half in range(2))
            for half in range(2):
                a3_w = keep.tile([P, P], U32, name=f"a3_w{b}{half}", align_bytes=64)
                a3_sc = keep.tile([P, P], U8, name=f"a3_sc{b}{half}", align_bytes=64)
                nc.vector.quantize_mx(
                    out=a3_w[:].bitcast(FP8X4), scales=a3_sc[:], in_=a3[b, half][:].rearrange("p j t -> p (j t)")
                )
                for m in range(N // P):
                    cols = slice(m * P, (m + 1) * P)
                    nc.tensor.matmul_mx(
                        out=y[half][:, m, :],
                        lhsT=w2_w[b][:, cols].bitcast(FP8X4), lhsT_scale=w2_sc[b][:, cols],
                        rhs=a3_w[:].bitcast(FP8X4), rhs_scale=a3_sc[:],
                        start=(b == 0 and m == 0), stop=(b == PASSES - 1 and m == N // P - 1),
                    )

        h, left, square, a1, first, second, a2, one, both = {}, {}, {}, {}, {}, {}, {}, {}, {}

        def first_product(s):
            h[s] = ring.tile([P, S], F32, name="h")
            acc = [psum.tile([P, BANK], F32, name="acc", tag="acc", bufs=4) for c in range(SLICES)]
            for c, a in itertools.product(range(SLICES), range(PASSES)):
                cols = slice(c * BANK, (c + 1) * BANK)
                words = v0[:, cols] if a == 0 else v1[c][:]
                nc.tensor.matmul_mx(
                    out=acc[c][:],
                    lhsT=w1_w[s][a].bitcast(FP4X4), lhsT_scale=w1_sc[s][a],
                    rhs=words.bitcast(FP8X4), rhs_scale=v_sc[a][:, cols],
                    start=(a == 0), stop=(a == PASSES - 1),
                )
                if a == PASSES - 1:
                    nc.scalar.activation(h[s][:, cols], acc[c][:], ACT.Sigmoid)

        def pick_left(s):
            left[s] = keep.tile([P, P1], F32, name="left", tag=f"picks{s % 2}")
            nc.vector.tensor_tensor(left[s][:], h[s][:].indirect(p1[:]), minus_one[:], ALU.mult)
            for half in range(2):
                square[s, half] = keep.tile([P, BANK], F32, name="square", tag=f"square{s % 3}{half}", align_bytes=64)
                nc.scalar.activation(square[s, half][:], left[s][:, half * BANK : (half + 1) * BANK], ACT.Square)

        def pick_right(s):
            cross = keep.tile([P, P1], F32, name="cross", tag=f"joins{s % 3}")
            nc.vector.tensor_tensor(cross[:], h[s][:].indirect(p2[:]), left[s][:], ALU.mult)
            turned = [
                keep.tile([P, BANK], F32, name="turned", tag=f"turned{s % 3}{half}", align_bytes=64) for half in range(2)
            ]
            a1[s] = keep.tile([P, P1], F32, name="a1", tag=f"joins{s % 3}")
            for half in range(2):
                cols = slice(half * BANK, (half + 1) * BANK)
                there = psum.tile([P, PACK, P], F32, name="there", bufs=2)
                for n, term in enumerate((square[s, half][:], cross[:, cols])):
                    for c in range(PACK):
                        blk = slice(c * P, (c + 1) * P)
                        nc.tensor.matmul(
                            there[:, c, :], term[:, blk], ident[:], is_transpose=True,
                            start=(n == 0 and c == 0), stop=(n == 1 and c == PACK - 1),
                        )
                nc.scalar.activation(turned[half][:], there[:].rearrange("p c r -> p (c r)"), ACT.Abs)
            for half in range(2):
                cols = slice(half * BANK, (half + 1) * BANK)
                back = psum.tile([P, PACK, P], F32, name="back", bufs=2)
                for c in range(PACK):
                    nc.tensor.transpose(back[:, c, :], turned[half][:, c * P : (c + 1) * P], ident[:])
                nc.scalar.copy(a1[s][:, cols], back[:].rearrange("p c r -> p (c r)"))

        def pick_first(s):
            first[s] = keep.tile([P, P2], F32, name="first", tag=f"picks{s % 2}")
            for j in range(0, P2, P3):
                nc.vector.tensor_copy(first[s][:, j : j + P3], a1[s][:].indirect(p3[:, j // 16 : (j + P3) // 16]))

        def pick_second(s):
            second[s] = ring.tile([P, P2], F32, name="second")
            nc.vector.tensor_copy(second[s][:], a1[s][:].indirect(p4[:]))

        def larger(s):
            a2[s] = ring.tile([P, P2], F32, name="a2")
            for j in range(0, P2, P3):
                cols = slice(j, j + P3)
                nc.vector.tensor_tensor(a2[s][:, cols], first[s][:, cols], second[s][:, cols], ALU.max)

        def pick_one(s):
            one[s] = ring.tile([P, P3], F32, name="one")
            nc.vector.tensor_copy(one[s][:], a2[s][:].indirect(p5[:]))

        def add_other(s):
            both[s] = ring.tile([P, P3], F32, name="both", bufs=5)
            width = P if s == SLOTS - 1 else P3
            for j in range(0, P3, width):
                cols = slice(j, j + width)
                places = p6[:, j // 16 : (j + width) // 16]
                nc.vector.tensor_tensor(both[s][:, cols], a2[s][:].indirect(places), one[s][:, cols], ALU.add)

        def apply_gain(s):
            b = s // PACK
            for half in range(2):
                if (b, half) not in a3:
                    tag = ("square", "turned")[b] + f"{(SLOTS - 1) % 3}{half}"
                    a3[b, half] = keep.tile([P, P, PACK], BF16, name=f"a3_{b}{half}", tag=tag, align_bytes=64)
                nc.scalar.activation(
                    a3[b, half][:, :, s % PACK], both[s][:, half * P : (half + 1) * P], ACT.Copy, scale=gain_t[:, s : s + 1]
                )

        lag = 3
        steps = (
            (pick_second, lag), (pick_first, lag), (pick_left, 0), (larger, lag),
            (pick_right, 0), (pick_one, lag), (add_other, lag),
        )
        first_product(0)
        for rnd in range(SLOTS + lag):
            if rnd + 1 < SLOTS:
                first_product(rnd + 1)
            for step, behind in steps:
                if 0 <= rnd - behind < SLOTS:
                    step(rnd - behind)
            if rnd in (6, 7):
                quantise_w2(rnd - 6)
            if rnd == SLOTS - 1:
                for s in range(PACK):
                    apply_gain(s)
            if rnd >= SLOTS - 1:
                apply_gain(rnd - lag)
            if rnd == SLOTS:
                second_product(0)
        second_product(1)

        out_rows = out.rearrange("(m p) j -> p m j", p=P)
        for half in range(2):
            cols = slice(half * P, (half + 1) * P)
            res = keep.tile([P, N // P, P], F32, name=f"res{half}")
            nc.vector.tensor_tensor(res[:], y[half][:], bar_t[:, :, cols], ALU.max)
            nc.sync.dma_start(out_rows[:, :, cols], res[:])
